import numpy as np, ml_dtypes
CORES = [242,247,114,119]
N = 4
BF = ml_dtypes.bfloat16
V, D, L, RO, HOP = 1536, 8, 192, 5, 2
def meet(rng, n, rest):
    p = np.argsort(rng.random((N, 8, n, V)), axis=-1); h = np.zeros_like(p)
    np.put_along_axis(h, p[..., 0::2], p[..., 1::2], 3); np.put_along_axis(h, p[..., 1::2], p[..., 0::2], 3)
    o = np.concatenate([h, rest], axis=2)
    return np.ascontiguousarray(np.take_along_axis(o, np.argsort(rng.random(o.shape), axis=2), 2))
def court(rng, lo, hi):
    c = rng.integers(0, V, (N, 8, V))
    for r in range(N):
        for g in range(8):
            h = int(rng.integers(3, 10)); chief = rng.permutation(V)[:h]; w = np.add.accumulate(np.exp2(-(0.1 + rng.random()) * np.arange(h)))
            j = np.minimum(np.searchsorted(w, rng.random(V) * w[-1], side="right"), h - 1)
            c[r, g] = np.where(rng.random(V) < lo + (hi - lo) * rng.random(), chief[j], c[r, g])
    return c
def hubs(rng, og, n):
    z = rng.permutation(V)[:RO * n]; vv = np.concatenate([D * rng.permutation(L)[:16 * n] + t for t in range(RO)]).reshape(RO * n, 16)
    og[rng.integers(0, 16, vv.shape), vv] = z[:, None]; og[:, z] = vv.T
    return z
def pack(o, x, c):
    return {"hol": np.ascontiguousarray(o.reshape(N, 128, V)).astype(np.int32), "sha": np.ascontiguousarray(x.reshape(N, 128, V)).astype(np.float32).astype(BF), "ctl": c.astype(np.int32)}
def setup_inputs(rng):
    o = meet(rng, 8, rng.integers(0, V, (N, 8, 8, V))); c = court(rng, 0.85, 0.95); x = rng.integers(0, 16, (N, 8, 16, V))
    for r in range(N):
        for g in range(8): hubs(rng, o[r, g], 2)
    return pack(o, x, c)
def setup_inputs_spread(rng):
    e = rng.integers(1, 7, (N, 8, 1, 1)); o = meet(rng, 8, np.minimum((V * rng.random((N, 8, 8, V)) ** e).astype(np.int64), V - 1))
    c = court(rng, 0.5, 1.0); q = np.minimum((V * rng.random((N, 8, V)) ** rng.integers(1, 9, (N, 8, 1))).astype(np.int64), V - 1)
    c = np.where(rng.random((N, 8, V)) < 0.15, q, c)
    x = np.minimum((rng.random((N, 8, 16, V)) * rng.choice(np.array([1, 2, 3, 6, 11, 16]), (N, 8, 1, V))).astype(np.int64), 15)
    return pack(o, x, c)
def setup_inputs_ends(rng):
    top = V - 1; p = rng.choice(np.array([0.15, 0.5, 0.85]), (N, 8, 1, V)); odd = np.arange(16) % 2
    o = meet(rng, 6, np.where(rng.random((N, 8, 10, V)) < p, top, 0)); c = top * rng.integers(0, 2, (N, 8, V)); kind = rng.random((N, 8, 1, V))
    x = 15 * np.where(kind < 0.45, 1, np.where(kind < 0.55, 0, rng.integers(0, 2, (N, 8, 16, V))))
    for r in range(N):
        for g in range(8):
            og, xg, cg = o[r, g], x[r, g], c[r, g]
            if g % 4 == 1: cg[0] = top; cg[top] = 0
            elif g % 4 != 3 or g == 7:
                cg[0] = 0; cg[top] = top; xg[:, 0] = 15; xg[:, top] = 15; og[:, 0] = top * odd
                for t in range(RO):
                    v = D * (L - 1) + t; og[:, v] = top; xg[:, v] = 15
                    v = D * (L - 2) + t; og[:, v] = top * odd; xg[:, v] = 15
                    v = D + t; og[:, v] = top * (1 - odd); xg[:, v] = 15
                    xg[:, 2 * D + t] = 0
                    v = D * (L - 3) + t; z = D * (L - 1 - 2 * t) + D - 2; og[:, v] = top; xg[:, v] = 15
                    for k, a in ((14, z), (15, z - D)): og[k, v] = a; og[15, a] = v; xg[:, a] = 0; cg[a] = 0
    return pack(o, x, c)
def setup_inputs_corners(rng):
    o = meet(rng, 8, rng.integers(0, V, (N, 8, 8, V))); c = court(rng, 0.8, 1.0); x = rng.integers(0, 16, (N, 8, 16, V)); own = np.arange(V)
    kind = rng.integers(0, 8, (N, 8, 1, V)); x = np.where(kind == 0, 0, np.where(kind == 1, 15, x))
    for r in range(N):
        mo, ho = rng.permutation(8), rng.permutation(8)
        for g in range(8):
            og = o[r, g]; m, h = int(mo[g]), int(ho[g])
            if m == 0: c[r, g] = own
            elif m == 1: c[r, g] = 0
            elif m == 2: c[r, g] = V - 1
            elif m == 3: c[r, g] = (own + 1) % V
            elif m == 4: c[r, g] = V - 1 - own
            elif m == 5: c[r, g] = np.choose(rng.integers(0, 3, V), [np.zeros_like(own), own, np.full_like(own, V - 1)])
            if h in (0, 4): og[rng.integers(0, 16, V), own] = own
            elif h == 1: one = rng.random(V) < 0.3; og[:, one] = og[:1, one]
            elif h == 2: og[:] = np.choose(rng.integers(0, 3, (16, V)), [np.zeros((16, V), np.int64), np.broadcast_to(own, (16, V)), np.full((16, V), V - 1)])
            elif h == 3: og[3] = (own + 1) % V; og[12] = (own - 1) % V
    return pack(o, x, c)
def setup_inputs_ties(rng):
    o = meet(rng, 8, rng.integers(0, V, (N, 8, 8, V))); x = rng.integers(14, 16, (N, 8, 16, V)); c = np.zeros((N, 8, V), np.int64); idle = np.flatnonzero(np.arange(V) % D >= RO)
    for g in range(8):
        f = rng.permutation(idle)[:3]; f = f[:2 + g % 2]
        for r in range(N):
            c[r, g] = f[rng.integers(0, 2, V)]
            if g % 2: c[r, g] = np.where(rng.random(V) < 0.1, f[2], c[r, g])
            c[r, g, f] = f
            if g % 4 == 1: x[r, g] = 15
            elif g % 4 == 2:
                n = 9 if g == 2 else int(rng.integers(8, 11)); x[r, g] = (rng.permutation(16) < n).astype(np.int64)[:, None] * rng.integers(1, 16, (16, 1))
            elif g % 4 == 3: x[r, g] -= 7
    return pack(o, x, c)
def setup_inputs_rush(rng):
    o = meet(rng, 8, rng.integers(0, V, (N, 8, 8, V))); x = rng.integers(6, 16, (N, 8, 16, V)); low = rng.integers(0, 4, (N, 8, 16, V)); c = np.zeros((N, 8, V), np.int64)
    act, idle = np.flatnonzero(np.arange(V) % D < RO), np.flatnonzero(np.arange(V) % D >= RO)
    for g in range(8):
        f = rng.permutation(idle)[:2]; tp = {5: 0, 7: RO - 1}.get(g, -1)
        if tp >= 0: f[0] = D * int(rng.integers(0, L)) + tp
        for r in range(N):
            og = o[r, g]; k = rng.integers(0, 16, V); c[r, g] = np.where(rng.random(V) < 0.8, f[0], f[1]); z = act
            if g % 4 == 0: z = hubs(rng, og, L // 16)
            elif g % 4 == 1:
                for t in range(RO):
                    q = D * rng.permutation(L) + t; a, b = q[0::2], q[1::2]; og[k[a], a] = b; og[k[b], b] = a
            elif g % 4 == 2:
                og[k[act], act] = act; h = act[rng.random(len(act)) < 0.5]; og[(k[h] + 5) % 16, h] = h
            else:
                n = min(len(act), len(idle)); a, z = rng.permutation(act)[:n], rng.permutation(idle)[:n]
                for j in range(5): og[(k[a] + j) % 16, a] = z; og[(k[z] + j) % 16, z] = a
            c[r, g, z] = f[1]; x[r, g][:, z] = low[r, g][:, z]
            c[r, g, f] = f; x[r, g][:, f[0]] = 15
            if tp >= 0:
                h, y = [int(e) for e in rng.permutation(idle[idle != f[1]])[:2]]; i1, i2 = [int(e) for e in rng.permutation(16)[:2]]
                v = D * ((int(f[0]) // D + 1 + int(rng.integers(0, L - 1))) % L) + tp
                og[:, v] = h; og[i1, v] = f[0]; og[i2, v] = y; og[int(rng.integers(0, 16)), y] = v
                og[:, f[0]] = h; og[int(rng.integers(0, 16)), f[0]] = v
                c[r, g, h] = f[0]; c[r, g, v] = f[1]; c[r, g, y] = f[1]; x[r, g][:, h] = 15; x[r, g][:, v] = rng.integers(1, 4, 16)
    return pack(o, x, c)
def check_inputs(d):
    bad = []
    for k, hi in (("hol", V - 1), ("sha", 15), ("ctl", V - 1)):
        v = np.asarray(d[k]).astype(np.float64)
        if not (np.min(v) >= 0 and np.max(v) <= hi): bad.append("range of " + k)
        elif np.any(v != np.floor(v)): bad.append("whole numbers of " + k)
    return bad
def reference(hol, sha, ctl):
    o = hol.astype(np.int64).reshape(N, 8, 16, V); x = sha.astype(np.float32).astype(np.int64).reshape(N, 8, 16, V); c = ctl.astype(np.int64)
    last = np.zeros(N, np.int64)
    for t in range(RO):
        d = 1 + t % (N - 1); vs = D * np.arange(L) + t
        no, nc, wins = [], [], []
        for r in range(N):
            a = o[r][:, :, vs]; af = a.reshape(8, 16 * L); cf = af
            for h in range(HOP): cf = np.take_along_axis(c[(r + h * d) % N], cf, 1)
            ck = cf.reshape(8, 16, L)
            xk = np.take_along_axis(x[r], af[:, None, :], 2).reshape(8, 16, 16, L); xv = x[r][:, :, vs]
            m = np.add.reduce(np.minimum(xk, xv[:, :, None, :]), axis=1)
            pool = np.add.reduce(np.where(ck[:, :, None, :] == ck[:, None, :, :], m[:, None, :, :], 0), axis=2)
            kb = np.argmax(pool, axis=1)
            b = np.take_along_axis(ck, kb[:, None, :], 1)[:, 0]
            mine = ck == b[:, None, :]
            part = np.add.reduce(np.where(mine[:, None, :, :], xk, 0), axis=2); full = np.add.reduce(xk, axis=2)
            win = np.add.reduce((2 * part > full).astype(np.int64), axis=1) >= 9 + (last[r] & 1)
            ok = np.take_along_axis(o[r], af[:, None, :], 2).reshape(8, 16, 16, L)
            stake = np.any(ok == vs, axis=1)
            xb = np.take_along_axis(x[r], b[:, None, :], 2)
            far = np.where(stake & ~mine, np.add.reduce(np.abs(xk - xb[:, :, None, :]), axis=1), -1)
            ks = np.argmax(far, axis=1); sells = win & (np.max(far, axis=1) >= 0)
            goal = np.take_along_axis(a, ks[:, None, :], 1)[:, 0]; cs = np.take_along_axis(ck, ks[:, None, :], 1)[:, 0]
            on = o[r] + 0; cn = c[r] + 0
            for g in range(8):
                ln = np.flatnonzero(sells[g]); tg, first = np.unique(goal[g, ln], return_index=True); w = ln[first]
                col = o[r, g][:, tg]; on[g][:, tg] = np.where(col == vs[w], cs[g, w], col)
                on[g, ks[g, ln], vs[ln]] = b[g, ln]
            cn[:, vs] = np.where(win, b, vs)
            no.append(on); nc.append(cn); wins.append(np.add.reduce(win.astype(np.int64).reshape(-1)))
        o = np.stack(no); c = np.stack(nc); last = np.array(wins, np.int64)
    return {"yo": o.reshape(N, 128, V).astype(np.float32), "yc": c.astype(np.float32)}

from concourse.mybir import AluOpType, AxisListType, ActivationFunctionType

A, AX, AF = AluOpType, AxisListType, ActivationFunctionType
V, L, NR = 1536, 192, 5
DD = [1, 2, 3, 1, 2]
LASTUSE = {1: 3, 2: 4, 3: 2}
B2, F4, I4, U2 = "bfloat16", "float32", "int32", "uint16"


def sb(*s, d=F4):
    return ("sbuf", list(s), d)


SCRATCH = {
    "hin": sb(128, V, d=I4), "cin": sb(128, 96, d=I4), "CO": sb(128, L, d=B2), "LC1": sb(128, L, d=B2), "LC2": sb(128, L, d=B2), "LC3": sb(128, L, d=B2),
    "Ow": sb(128, V + L), "Xw": sb(128, V, d=B2),
    "W0": sb(128, V, d=B2), "W1": sb(128, V, d=B2), "W2": sb(128, V, d=B2), "W3": sb(128, V, d=B2), "CC": sb(128, V, d=B2), "CL": sb(128, 96, d=U2),
    "off": sb(128, L, d=U2), "Fx": sb(128, 12, 256, d=B2), "Fc": sb(128, 12, 256, d=B2), "Fc2": sb(128, 4096, d=B2),
    "Eo": sb(128, 12, 256, d=B2), "FM": sb(128, 12, 256, d=B2), "prod": sb(128, 16, L, d=B2),
    "vx": sb(128, 16 * L), "ln8": sb(128, L),
    "csb": sb(128, 12, 24), "msb": sb(128, 12, 16, d=B2), "E": sb(128, 96, 16, d=B2), "Y1": sb(128, 96, 16, d=B2),
    "Y2": sb(128, 84, 16, d=B2), "kmx": sb(128, 12, d=I4), "kan": sb(128, 12, d=I4), "bof": sb(128, 12, d=U2),
    "bc": sb(128, L, d=B2), "cK": sb(128, L), "mK": sb(128, L, d=B2), "mm": sb(128, L, d=B2),
    "bT": sb(128, 12), "bTu": sb(128, 12, d=U2), "xb": sb(128, L, d=B2),
    "bexp": sb(128, 12, 16), "nm": sb(128, 12, 16), "cb": sb(128, 12, 16), "sk": sb(128, 12, 16),
    "sof": sb(128, 12, d=U2), "ohk": sb(128, L, d=B2),
    "wb": sb(128, L, d=B2), "cvb": sb(128, L, d=B2), "cv": sb(128, L, d=B2), "dd": sb(128, L),
    "aD": sb(128, L), "Ap": sb(128, L), "gb": sb(128, 12, 16), "gT": sb(128, 12), "gTu": sb(128, 12, d=U2),
    "Eb": sb(128, 144, 16, d=B2), "Ed": sb(128, 12, 16, d=B2), "D2": sb(128, 12, 16), "sT": sb(128, 12), "slu": sb(128, 12, d=U2),
    "csc": sb(128, L, d=B2), "col": sb(128, L), "e1": sb(128, L), "ox": sb(128, L),
    "wc": sb(128, 1), "w12": sb(128, 12), "Z": sb(128, 1),
    "pmi": sb(128, 1, d=I4), "pma": sb(128, 1, d=I4), "pmb": sb(128, 1, d=I4), "pm": sb(128, 1), "lt": sb(128, 1), "lo": sb(128, 1), "hi": sb(128, 1), "wr": sb(128, 1),
    "iq": sb(128, 16), "rs": sb(128, 16), "iq3": sb(128, 12, 16), "dl": sb(128, 12, 16), "dlb": sb(128, L, d=B2), "dum": sb(128, L), "dmk": sb(128, 12, 16), "tri": sb(128, 12, 16, d=B2),
    "lnq": sb(128, L), "lT": sb(128, 12, 16), "lT2": sb(128, 12, 16), "K1": sb(128, 12, 16, d=B2), "K2": sb(128, 12, 16, d=B2),
    "one": sb(128, 128), "G1": sb(128, 128), "Gf": sb(128, 128), "If": sb(128, 128), "G": sb(128, 128, d=B2), "Gc": sb(128, 128, d=B2), "Gn": sb(128, 128, d=B2), "G2k": sb(128, 128, d=B2), "R0": sb(128, 128),
    "I1": sb(128, 128, d=B2), "In": sb(128, 128, d=B2), "I16": sb(128, 128, d=B2), "I4k": sb(128, 128, d=B2),
    "Sel": sb(128, 16, 128, d=B2), "Sec": sb(128, 16, 128, d=B2), "BE": sb(128, 16, 128, d=B2),
    "SeA": sb(128, 16, 128, d=B2), "SeC": sb(128, 16, 128, d=B2),
    "woh": sb(128, 4096, d=B2), "ycb": sb(128, V),
    "PA": ("psum", [128, 16, 32], F4), "PB": ("psum", [128, 16, 32], F4), "PC": ("psum", [128, 32, 16], F4), "PD": ("psum", [128, 32, 16], F4),
    "PE": ("psum", [128, 32, 16], F4), "PG": ("psum", [128, 32, 16], F4), "PH": ("psum", [128, 32, 16], F4), "PX": ("psum", [128, 32, 16], F4),
}
for _t in range(NR):
    SCRATCH["Cb%d" % _t] = sb(128, L, d=B2)
LAND = [(d, t) for d in (1, 2, 3) for t in range(LASTUSE[d])]
for _d, _t in LAND:
    SCRATCH["L%d%d" % (_d, _t)] = sb(128, L, d=B2)
SEMAPHORES = ["v", "t", "s", "p", "dh", "dx", "dc", "d0", "d1", "d2", "d3", "dw", "dy", "dz", "ls", "l0"] + ["i%d" % d for d in (1, 2, 3)] + ["a%d%d" % x for x in LAND]


def rank_program(g, core, T, topo):
    rank = T.rank_of(core)
    if rank is None:
        return
    Q = {"v": g.vector, "t": g.tensor, "s": g.scalar, "p": g, "y": g.sync}
    cnt = {k: 0 for k in Q}
    known = {k: {} for k in Q}
    snap, writer, readers, bank = {}, {}, {}, {}

    def need(q, toks):
        kn = known[q]
        for s, n in sorted(toks, key=lambda x: -x[1]):
            if kn.get(s, 0) >= n:
                continue
            Q[q].wait_ge(T.sem[s], n)
            kn[s] = n
            for a, b in snap.get((s, n), {}).items():
                if kn.get(a, 0) < b:
                    kn[a] = b

    def op(q, fn, r=(), w=(), b=(), dma=None, amt=1):
        toks = set()
        for x in r:
            if x not in writer:
                raise ValueError("read before write: " + x)
            toks.add(writer[x])
        for x in w:
            if x in writer and writer[x][0] != q:
                toks.add(writer[x])
            for e, n in readers.get(x, {}).items():
                if e != q:
                    toks.add((e, n))
        for x in b:
            for e, n in bank.get(x, {}).items():
                if e != q:
                    toks.add((e, n))
        need(q, toks)
        if dma:
            cnt[dma] = cnt.get(dma, 0) + amt
            tok = (dma, cnt[dma])
        else:
            cnt[q] += 1
            tok = (q, cnt[q])
        snap[tok] = dict(known[q])
        fn().then_inc(T.sem[tok[0]], amt)
        for x in r:
            readers.setdefault(x, {})[tok[0]] = tok[1]
        for x in w:
            writer[x] = tok
            readers[x] = {}
        for x in b:
            bank.setdefault(x, {})[tok[0]] = tok[1]

    def R(n, *ks):
        return [n + str(k) for k in range(*ks)]

    def TT(o, a, c, f, **k):
        op("v", lambda: g.vector.tensor_tensor(o, a, c, f), **k)

    def TS(o, a, s1, f1, s2=None, f2=None, **k):
        if f2 is None:
            op("v", lambda: g.vector.tensor_scalar(o, a, s1, None, f1), **k)
        else:
            op("v", lambda: g.vector.tensor_scalar(o, a, s1, s2, f1, f2), **k)

    def CP(o, a, **k):
        op("v", lambda: g.vector.tensor_copy(o, a), **k)

    def RED(o, a, f, **k):
        op("v", lambda: g.vector.tensor_reduce(o, a, AX.X, f), **k)

    def MS(o, c, **k):
        op("v", lambda: g.vector.memset(o, c), **k)

    def SC(o, a, bias=None, **k):
        if bias is None:
            op("s", lambda: g.scalar.activation(o, a, AF.Copy), **k)
        else:
            op("s", lambda: g.scalar.activation(o, a, AF.Identity, bias=bias), **k)

    def MM(o, l, r_, st, sp, **k):
        op("t", lambda: g.tensor.matmul(o, l, r_, st, sp), **k)

    def IO(o, pat, base, cm, **k):
        op("p", lambda: g.iota(o, pat, base, cm, allow_small_or_imprecise_dtypes=True), **k)

    op("s", lambda: g.scalar.dma_start(T.cin[:], T.ctl[:]), w=["cin"], dma="dc", amt=16)
    op("y", lambda: g.sync.dma_start(T.hin[:], T.hol[:]), w=["hin"], dma="dh", amt=16)
    op("s", lambda: g.scalar.dma_start(T.Xw[:], T.sha[:]), w=["Xw"], dma="dx", amt=16)

    MS(T.one[:], 1.0, w=["one"])
    for d in (0, 1):
        MS(T["W%d" % d][:], 0.0, w=["W%dz" % d])
    MS(T.Sec[:], 0.0, w=R("Sec", 16))
    MS(T.Sel[:], 0.0, w=R("Sel", 16))
    IO(T.pmi[:], [[0, 1]], 0, 1, w=["pmi"])
    op("p", lambda: g.affine_select(T.G1[:], T.one[:], [[-16, 8], [0, 16]], A.is_ge, 0.0, 0, 1), r=["one"], w=["G1"])
    op("p", lambda: g.affine_select(T.Gf[:], T.G1[:], [[16, 8], [0, 16]], A.is_ge, 0.0, 15, -1), r=["G1"], w=["Gf"])
    op("p", lambda: g.affine_select(T.If[:], T.one[:], [[-1, 128]], A.is_equal, 0.0, 0, 1), r=["one"], w=["If"])
    for d in (2, 3):
        SC(T["W%d" % d][:], T.W1[:], r=["W1z"], w=["W%dz" % d])
    CP(T.CO[:, 0:96], T.cin[:], r=["cin"], w=["COa"])
    TT(T.CO[:, 96:L], T.cin[:], T.CO[:, 0:96], A.subtract, r=["cin", "COa"], w=["CO"])
    TS(T.pma[:], T.pmi[:], 15, A.bitwise_and, r=["pmi"], w=["pma"])
    TS(T.pmb[:], T.pmi[:], 1, A.bitwise_and, r=["pmi"], w=["pmb"])
    CP(T.pm[:], T.pma[:], r=["pma"], w=["pm"])
    CP(T.lo[:], T.pmb[:], r=["pmb"], w=["lo"])

    sem_of = {}
    peers = {d: T.cores[(rank - d) % 4] for d in (1, 2, 3)}
    nls = {"ls": 0, "l0": 0}

    def send(dst, src_t, dst_t, sem, r, ls="ls"):
        need("p", [writer[r]])
        rid, pid = topo.addr(dst, core)
        es = topo.engines(core, dst)[:8]
        nls[ls] += len(es)
        g.remote_dma(dst_t, src_t, T.sem[sem], T.sem[ls], pid, rid, sum(1 << e for e in es))

    def arrive(src, sem, tag):
        n = len(topo.engines(src, core)[:8])
        sem_of[tag] = (sem, n)
        writer[tag] = (sem, n)

    for d in (1, 2, 3):
        send(peers[d], T.CO[:], T["LC%d" % d][:], "i%d" % d, "CO", "l0")
        arrive(T.cores[(rank + d) % 4], "i%d" % d, "LC%d" % d)
    for d, t in LAND:
        arrive(T.cores[(rank + d) % 4], "a%d%d" % (d, t), "L%d%d" % (d, t))

    def spread(d, src, tag):
        Wd, wd, sm = T["W%d" % d], "W%d" % d, "d%d" % d
        op("y", lambda: g.sync.dma_start(Wd[0::16, :], src[:, 0:96]), r=[tag, wd + "z"], w=[wd + "z"], dma=sm, amt=16)
        op("y", lambda: g.sync.dma_start(Wd[1::16, :], src[:, 96:L]), r=[tag], dma=sm, amt=16)
        writer[wd] = (sm, 32)

    IO(T.iq[:], [[1, 16]], 0, 0, w=["iq"])
    IO(T.iq3[:], [[0, 12], [1, 16]], 0, 0, w=["iq3"])
    IO(T.lT[:], [[16, 12], [0, 16]], 0, 0, w=["lT"])
    IO(T.vx[:], [[8, L], [0, 16]], 0, 0, w=["vx"])
    IO(T.lnq[:], [[1, L]], 0, 0, w=["lnq"])
    IO(T.ln8[:], [[8, L]], 0, 0, w=["ln8"])
    IO(T.woh[:, 3072:4096], [[0, 1024]], 0, 0, w=["wohz"])
    IO(T.Fc2[:, 3072:4096], [[0, 1024]], 0, 0, w=["F2Z"])
    IO(T.Ow[:, V:V + L], [[0, L]], 0, 0, w=["Owd"])
    spread(0, T.CO, "CO")
    spread(1, T.LC1, "LC1")

    def offcast(t, src, tag):
        CP(T.off[:], src[:, t:V:8], r=[tag], w=["off"])

    CP(T.G[:], T.Gf[:], r=["Gf"], w=["G"])
    TS(T.wr[:], T.pm[:], 2.0, A.is_lt, r=["pm"], w=["wr"])
    TS(T.Gc[:], T.Gf[:], T.wr[:], A.mult, r=["Gf", "wr"], w=["Gc"])
    for q in range(16):
        SC(T.Sec[:, q, q::16], T.Gc[:, q::16], r=["Gc"], w=["Sec%d" % q])
    for q in range(16):
        CP(T.Sel[:, q, q::16], T.G[:, q::16], r=["G"], w=["Sel%d" % q])
    SELS = R("Sel", 16)
    CP(T.I1[:], T.If[:], r=["If"], w=["I1"])
    TS(T.I16[:], T.If[:], 16.0, A.mult, r=["If"], w=["I16"])
    TS(T.I4k[:], T.If[:], 4096.0, A.mult, r=["If"], w=["I4k"])
    TS(T.lT2[:], T.lT[:], T.pm[:], A.add, r=["lT", "pm"], w=["lT2"])
    TS(T.K1[:], T.lT2[:], -1.0, A.mult, 255.0, A.add, r=["lT2"], w=["K1"])
    TS(T.K2[:], T.iq3[:], -1.0, A.mult, 15.0, A.add, r=["iq3"], w=["K2"])
    offcast(0, T.hin, "hin")
    CP(T.Ow[:, 0:V], T.hin[:], r=["hin"], w=["Ow"])

    def consts_pool():
        TS(T.SeC[:], T.Sel[:], 4194304.0, A.mult, r=SELS, w=["SeC"])
        TS(T.dl[:], T.iq3[:], T.pm[:], A.is_equal, r=["iq3", "pm"], w=["dl"])
        CP(T.dlb[:], T.dl[:], r=["dl"], w=["dlb"])
        for j in range(16):
            op("y", lambda: g.sync.dma_start(T.woh[:, L * j:L * j + L], T.dlb[:]), r=["dlb"], dma="dw", amt=16)
        writer["woh"] = ("dw", 256)
        TS(T.rs[:], T.iq[:], T.pm[:], A.is_equal, r=["iq", "pm"], w=["rs"])
        for k in range(16):
            TS(T.BE[:, k, :], T.G[:], T.rs[:, k:k + 1], A.mult, r=["G", "rs"], w=["BE%d" % k])
        MS(T.Z[:], 9.0, w=["Z"])
        for d in (2, 3):
            spread(d, T["LC%d" % d], "LC%d" % d)
        TS(T.In[:], T.If[:], -1.0, A.mult, r=["If"], w=["In"])
        TS(T.hi[:], T.lo[:], -1.0, A.mult, 1.0, A.add, r=["lo"], w=["hi"])
        TS(T.cvb[:], T.ln8[:], T.hi[:], A.mult, r=["ln8", "hi"], w=["cvb"])
        TS(T.dum[:], T.lnq[:], 1536.0, A.add, r=["lnq"], w=["dum"])

    def consts_sale():
        TT(T.dmk[:], T.dum[:], T.dl[:], A.mult, r=["dum", "dl"], w=["dmk"])
        TS(T.tri[:], T.iq3[:], T.pm[:], A.is_gt, r=["iq3", "pm"], w=["tri"])
        TS(T.Gn[:], T.Gc[:], -1.0, A.mult, r=["Gc"], w=["Gn"])
        TS(T.G2k[:], T.G[:], 2048.0, A.mult, r=["G"], w=["G2k"])
        TS(T.wr[:], T.pm[:], 0.0, A.is_equal, r=["pm"], w=["wr"])
        TS(T.R0[:], T.one[:], T.wr[:], A.mult, r=["one", "wr"], w=["R0"])

    def compose(t, q):
        d = DD[t]
        wn = "W%d" % d
        for t0 in range(t):
            tag = "L%d%d" % (d, t0)
            if tag in sem_of and DD[t0 + 1:t + 1].count(d) == 1:
                SC(T[wn][:, t0:V:8], T[tag][:], r=[tag], w=[wn])
        (CP if q == "v" else SC)(T.CC[:], T[wn][:].indirect(T.CL[:]), r=[wn, "CL"], w=["CC"])

    def cl_sum():
        for q in range(16):
            MM(T.PX[:, 12:18, :], T.Sec[:, q, :], T.W0[:, q::16], q == 0, q == 15, r=["W0", "Sec%d" % q], w=["CLp"], b=["PX"])

    def cl_list():
        CP(T.CL[:], T.PX[:, 12:18, :], r=["CLp"], w=["CL"], b=["PX"])

    def rule():
        CP(T.pma[:], T.PG[:, 24, 0:1], r=["tot"], w=["pma"], b=["PG"])
        TS(T.pmb[:], T.pma[:], 1, A.bitwise_and, r=["pma"], w=["pmb"])
        TS(T.Z[:], T.pmb[:], 9.0, A.add, r=["pmb"], w=["Z"])

    def eqo(a, b):
        for l in range(a, b):
            TT(T.Eo[:, l, :], T.Ow[:, 0:V].indirect(T.off[:, 16 * l:16 * l + 16]), T.vx[:, 256 * l:256 * l + 256], A.is_equal, r=["Ow", "off", "vx"], w=["Eo%d" % l])

    def fc(l, q):
        (CP if q == "v" else SC)(T.Fc[:, l, :], T.CC[:].indirect(T.off[:, 16 * l:16 * l + 16]), r=["CC", "off"], w=["Fc%d" % l])

    ZS = [(0, 8), (8, 12)]
    FCV, FCS, EQ = range(0, 4), range(4, 12), 3

    def mins(z):
        a, b = ZS[z]
        for k in range(16):
            TT(T.FM[:, a:b, k::16], T.Fx[:, a:b, k::16], T.PX[:, a:b, :], A.min, r=R("Fx", a, b) + ["xv"], w=["FM%d" % z], b=["PX"])

    def msum(z):
        a, b = ZS[z]
        for q in range(16):
            MM(T.PB[:, a:b, 0:16], T.Sel[:, q, :], T.FM[:, a:b, 16 * q:16 * q + 16], q == 0, q == 15, r=["FM%d" % z, "Sel%d" % q], w=["m"], b=["PB"])

    def stake(z):
        a, b = ZS[z]
        for q in range(16):
            MM(T.PE[:, a:b, :], T.SeC[:, q, :], T.Eo[:, a:b, 16 * q:16 * q + 16], q == 0, q == 15, r=R("Eo", a, b) + ["SeC"], w=["stk"], b=["PE"])

    def ck(j):
        for k in range(16):
            MM(T.PE[:, 12 + j:16 + j, :], T.Sec[:, k, :], T.Fc[:, j:j + 4, k::16], k == 0, k == 15, r=R("Fc", j, j + 4) + ["Sec%d" % k], w=["cKp"], b=["PE"])

    def csum(j):
        for q in range(16):
            MM(T.PA[:, j:j + 4, 0:16], T.Sec[:, q, :], T.Fc[:, j:j + 4, 16 * q:16 * q + 16], q == 0, q == 15, r=R("Fc", j, j + 4) + ["Sec%d" % q], w=["c"], b=["PA"])

    def far(z):
        a, b = ZS[z]
        for k in range(16):
            TT(T.FM[:, a:b, k::16], T.Fx[:, a:b, k::16], T.PH[:, a:b, :], A.subtract, r=R("Fx", a, b) + ["xbp"], w=["FM%d" % z], b=["PH"])

    def farmm(z):
        a, b = ZS[z]
        fm = T.FM[:, a:b, :]
        op("s", lambda: g.scalar.activation(fm, fm, AF.Abs), r=["FM%d" % z], w=["FM%d" % z])
        for q in range(16):
            MM(T.PD[:, a:b, :], T.SeA[:, q, :], T.FM[:, a:b, 16 * q:16 * q + 16], False, q == 15 and z == 1, r=["FM%d" % z, "SeA"], w=["skey"], b=["PD"])

    SC(T.PX[:, 0:12, :], T.Xw[:, 0:V:8], r=["Xw"], w=["xv"], b=["PX"])
    pend = []
    for t in range(NR):
        last = t == NR - 1
        for l in range(12):
            SC(T.Fx[:, l, :], T.Xw[:].indirect(T.off[:, 16 * l:16 * l + 16]), r=["Xw", "off"], w=["Fx%d" % l])
        if t == 0:
            cl_sum()
        MM(T.PC[:, 0:12, :], T.I16[:], T.K1[:], True, False, r=["I16", "K1"], w=["key"], b=["PC"])
        MM(T.PC[:, 0:12, :], T.I1[:], T.K2[:], False, False, r=["I1", "K2"], w=["key"], b=["PC"])
        MM(T.PD[:, 0:12, :], T.I16[:], T.K1[:], True, False, r=["I16", "K1"], w=["skey"], b=["PD"])
        MM(T.PD[:, 0:12, :], T.I1[:], T.K2[:], False, False, r=["I1", "K2"], w=["skey"], b=["PD"])
        if t == 0:
            cl_list()
            compose(0, "v")
        for l in FCV:
            fc(l, "v")
        for l in FCS:
            fc(l, "s")
        if t == 0:
            consts_pool()
        else:
            pend.pop()()
        eqo(0, EQ)
        mins(0)
        eqo(EQ, 12)
        mins(1)
        if not last:
            IO(T.vx[:], [[8, L], [0, 16]], t + 1, 0, w=["vx"])
        if t > 0:
            rule()
        csum(0)
        ck(0)
        msum(0)
        csum(4)
        ck(4)
        csum(8)
        msum(1)
        ck(8)
        SC(T.csb[:, :, 0:16], T.PA[:, 0:12, 0:16], r=["c"], w=["csb"], b=["PA"])
        SC(T.csb[:, :, 16:24], T.PA[:, 0:12, 0:8], r=["c"], w=["csb2"], b=["PA"])
        SC(T.Fc2[:, 0:3072], T.Fc[:], r=R("Fc", 12), w=["F2D"])
        for s in range(1, 9):
            TT(T.E[:, 12 * s - 12:12 * s, :], T.csb[:, :, s:s + 16], T.PA[:, 0:12, 0:16], A.is_equal, r=["c", "csb", "csb2"], w=["E%d" % s], b=["PA"])
        CP(T.PB[:, 0:12, 16:24], T.PB[:, 0:12, 0:8], r=["m"], w=["m2"], b=["PB"])
        CP(T.msb[:], T.PB[:, 0:12, 0:16], r=["m"], w=["msb"], b=["PB"])
        SC(T.cK[:], T.PE[:, 12:24, :], r=["cKp"], w=["cK"], b=["PE"])
        MM(T.PC[:, 0:12, :], T.I4k[:], T.msb[:], False, False, r=["I4k", "msb"], w=["key"], b=["PC"])
        for s in range(1, 9):
            e, y1 = T.E[:, 12 * s - 12:12 * s, :], T.Y1[:, 12 * s - 12:12 * s, :]
            if s < 8:
                TT(T.Y2[:, 12 * s - 12:12 * s, :], e, T.PB[:, 0:12, 0:16], A.mult, r=["E%d" % s, "m"], w=["Y2%d" % s], b=["PB"])
                MM(T.PC[:, 0:12, s:16], T.I4k[:], T.Y2[:, 12 * s - 12:12 * s, 0:16 - s], False, False, r=["I4k", "Y2%d" % s], w=["key"], b=["PC"])
                MM(T.PC[:, 0:12, 0:s], T.I4k[:], T.Y2[:, 12 * s - 12:12 * s, 16 - s:16], False, False, r=["I4k", "Y2%d" % s], w=["key"], b=["PC"])
            TT(y1, e, T.PB[:, 0:12, s:s + 16], A.mult, r=["E%d" % s, "m", "m2"], w=["Y1%d" % s], b=["PB"])
            MM(T.PC[:, 0:12, :], T.I4k[:], y1, False, s == 8, r=["I4k", "Y1%d" % s], w=["key"], b=["PC"])
        RED(T.kmx[:], T.PC[:, 0:12, :], A.max, r=["key"], w=["kmx"], b=["PC"])
        TS(T.kan[:], T.kmx[:], 4095, A.bitwise_and, r=["kmx"], w=["kan"])
        TS(T.bof[:], T.kan[:], -1.0, A.mult, 4095.0, A.add, r=["kan"], w=["bof"])
        CP(T.bc[:], T.Fc2[:].indirect(T.bof[:]), r=["F2D", "F2Z", "bof"], w=["bc"])
        stake(1)
        MM(T.PG[:, 0:12, :], T.Gc[:], T.bc[:], True, True, r=["Gc", "bc"], w=["b"], b=["PG"])
        TS(T.lt[:], T.lo[:], float(t), A.mult, r=["lo"], w=["lt"])
        TS(T.cv[:], T.cvb[:], T.lt[:], A.add, r=["cvb", "lt"], w=["cv"])
        TT(T.aD[:], T.Ow[:, t:V:8], T.dum[:], A.subtract, r=["Ow", "dum"], w=["aD"])
        TT(T.D2[:], T.PG[:, 0:12, :], T.dl[:], A.mult, r=["b", "dl"], w=["D2"], b=["PG"])
        TT(T.mK[:], T.cK[:], T.PG[:, 0:12, :], A.is_equal, r=["b", "cK"], w=["mK"], b=["PG"])
        RED(T.bT[:], T.D2[:], A.add, r=["D2"], w=["bT"])
        TS(T.mm[:], T.mK[:], 2.0, A.mult, -1.0, A.add, r=["mK"], w=["mm"])
        CP(T.bTu[:], T.bT[:], r=["bT"], w=["bTu"])
        SC(T.xb[:], T.Xw[:].indirect(T.bTu[:]), r=["Xw", "bTu"], w=["xb"])
        SC(T.PH[:, 0:12, :], T.xb[:], r=["xb"], w=["xbp"], b=["PH"])
        SC(T.bexp[:, :, 0], T.bT[:], r=["bT"], w=["bx0"])
        SC(T.bexp[:, :, 1], T.bT[:], r=["bT"], w=["bx1"])
        SC(T.bexp[:, :, 2:4], T.bexp[:, :, 0:2], r=["bx0", "bx1"], w=["bx2"])
        SC(T.bexp[:, :, 4:8], T.bexp[:, :, 0:4], r=["bx0", "bx1", "bx2"], w=["bx3"])
        SC(T.bexp[:, :, 8:16], T.bexp[:, :, 0:8], r=["bx0", "bx1", "bx2", "bx3"], w=["bx4"])
        MM(T.PB[:, 0:6, :], T.I1[:], T.bc[:], True, False, r=["I1", "bc"], w=["ddp"], b=["PB"])
        MM(T.PB[:, 0:6, :], T.In[:], T.cv[:], False, True, r=["In", "cv"], w=["ddp"], b=["PB"])
        SC(T.dd[:], T.PB[:, 0:6, :], r=["ddp"], w=["dd"], b=["PB"])
        rb = [("PC", T.PC), ("PX", T.PX)]
        for k in range(16):
            bn, bk = rb[(k // 2) % 2]
            z = 12 * (k % 2)
            MM(bk[:, z:z + 12, :], T.BE[:, k, :], T.mm[:], True, True, r=["mm", "BE%d" % k], w=["rg%d" % (k % 4)], b=[bn])
            if k % 2:
                for k2 in (k - 1, k):
                    z = 12 * (k2 % 2)
                    TT(T.prod[:, k2, :], T.Fx[:, :, k2::16], bk[:, z:z + 12, :], A.mult, r=R("Fx", 12) + ["rg%d" % (k2 % 4)], w=["pr%d" % k2], b=[bn])
        for k in range(16):
            MM(T.PB[:, 0:6, :], T.I1[:], T.prod[:, k, :], k == 0, k == 15, r=["pr%d" % k, "I1"], w=["wp"], b=["PB"])
        SC(T.PX[:, 18:30, :], T.ln8[:], bias=float(t), r=["ln8"], w=["vn"], b=["PX"])
        if t == 0:
            TS(T.SeA[:], T.Sel[:], 4096.0, A.mult, r=SELS, w=["SeA"])
        far(0)
        TS(T.wb[:], T.PB[:, 0:6, :], 0.0, A.is_gt, r=["wp"], w=["wb"], b=["PB"])
        MM(T.PB[:, 6:12, :], T.G[:], T.wb[:], True, True, r=["G", "wb"], w=["cn"], b=["PB"])
        far(1)
        stake(0)
        farmm(0)
        if t == 0:
            consts_sale()
        TT(T.nm[:], T.PA[:, 0:12, 0:16], T.bexp[:], A.not_equal, r=["c"] + R("bx", 5), w=["nm"], b=["PA"])
        TS(T.PH[:, 12:24, :], T.PB[:, 6:12, :], T.Z[:], A.is_ge, r=["cn", "Z"], w=["win"], b=["PB", "PH"])
        TT(T.PB[:, 0:6, :], T.dd[:], T.PH[:, 12:24, :], A.mult, r=["dd", "win"], w=["t1"], b=["PH", "PB"])
        farmm(1)
        CB = "Cb%d" % t
        TT(T[CB][:], T.PB[:, 0:6, :], T.cv[:], A.add, r=["t1", "cv"], w=[CB], b=["PB"])
        if t == 0:
            readers["W0"] = dict(readers.get("W0", {}))
        SC(T.W0[:, t:V:8], T[CB][:], r=[CB], w=["W0"])
        if not last:
            for dn in sorted((1, 2, 3), key=lambda x: x != DD[t + 1]):
                if (dn, t) in LAND:
                    send(peers[dn], T[CB][:], T["L%d%d" % (dn, t)][:], "a%d%d" % (dn, t), CB)
            RED(T.w12[:], T.PH[:, 12:24, :], A.add, r=["win"], w=["w12"], b=["PH"])
            cl_sum()
        TT(T.cb[:], T.PE[:, 0:12, :], T.nm[:], A.mult, r=["stk", "nm"], w=["cb"], b=["PE"])
        MM(T.PC[:, 0:12, :], T.If[:], T.dum[:], True, False, r=["If", "dum"], w=["goal"], b=["PC"])
        TT(T.sk[:], T.PD[:, 0:12, :], T.cb[:], A.min, r=["skey", "cb"], w=["sk"], b=["PD"])
        RED(T.kmx[:], T.sk[:], A.max, r=["sk"], w=["kmx"])
        TS(T.kan[:], T.kmx[:], 4095, A.bitwise_and, r=["kmx"], w=["kan"])
        TS(T.sof[:], T.kan[:], -1.0, A.mult, 4095.0, A.add, r=["kan"], w=["sof"])
        CP(T.ohk[:], T.woh[:].indirect(T.sof[:]), r=["woh", "wohz", "sof"], w=["ohk"])
        SC(T.csc[:], T.Fc2[:].indirect(T.sof[:]), r=["F2D", "F2Z", "sof"], w=["csc"])
        TT(T.PG[:, 12:24, :], T.ohk[:], T.PH[:, 12:24, :], A.mult, r=["ohk", "win"], w=["oh"], b=["PH", "PG"])
        TT(T.Ap[:], T.aD[:], T.PG[:, 12:24, :], A.mult, r=["aD", "oh"], w=["Ap"], b=["PG"])
        MM(T.PC[:, 0:12, :], T.Gf[:], T.Ap[:], False, True, r=["Gf", "Ap"], w=["goal"], b=["PC"])
        MM(T.PA[:, 0:6, :], T.Gn[:], T.cv[:], True, False, r=["Gn", "cv"], w=["dcs"], b=["PA"])
        MM(T.PA[:, 0:6, :], T.Gc[:], T.csc[:], False, True, r=["Gc", "csc"], w=["dcs"], b=["PA"])
        MM(T.PD[:, 12:24, :], T.If[:], T.dum[:], True, False, r=["If", "dum"], w=["goal2"], b=["PD"])
        MM(T.PD[:, 12:24, :], T.Gf[:], T.Ap[:], False, False, r=["Gf", "Ap"], w=["goal2"], b=["PD"])
        if not last:
            cl_list()
        TT(T.D2[:], T.PC[:, 0:12, :], T.dl[:], A.mult, r=["goal", "dl"], w=["D2"], b=["PC"])
        SC(T.gb[:], T.PC[:, 0:12, :], r=["goal"], w=["gb"], b=["PC"])
        RED(T.gT[:], T.D2[:], A.add, r=["D2"], w=["gT"])
        if not last:
            SC(T.PX[:, 0:12, :], T.Xw[:, t + 1:V:8], r=["Xw"], w=["xv"], b=["PX"])
            compose(t + 1, "s")
        CP(T.gTu[:], T.gT[:], r=["gT"], w=["gTu"])
        for l in range(12):
            TS(T.Eb[:, 13 * l:12 * l + 12, :], T.gb[:, l:12, :], T.gT[:, l:l + 1], A.is_equal, r=["gb", "gT"], w=["Eb%d" % l])
        TT(T.Ed[:], T.Eb[:, 0:144:13, :], T.tri[:], A.mult, r=R("Eb", 12) + ["tri"], w=["Ed"])
        for l in range(11):
            MM(T.PD[:, 13 + l:24, :], T.G2k[:], T.Eb[:, 13 * l + 1:12 * l + 12, :], False, False, r=["Eb%d" % l, "G2k"], w=["goal2"], b=["PD"])
        MM(T.PD[:, 12:24, :], T.G2k[:], T.Ed[:], False, True, r=["Ed", "G2k"], w=["goal2"], b=["PD"])
        CP(T.col[:], T.Ow[:].indirect(T.gTu[:]), r=["Ow", "Owd", "gTu"], w=["col"])
        TT(T.e1[:], T.col[:], T.PX[:, 18:30, :], A.is_equal, r=["col", "vn"], w=["e1"], b=["PX"])
        TT(T.PA[:, 0:6, :], T.e1[:], T.PA[:, 0:6, :], A.mult, r=["e1", "dcs"], w=["e2"], b=["PA"])
        TT(T.D2[:], T.PD[:, 12:24, :], T.dmk[:], A.min, r=["goal2", "dmk"], w=["D2"], b=["PD"])
        TT(T.ox[:], T.PA[:, 0:6, :], T.col[:], A.add, r=["e2", "col"], w=["ox"], b=["PA"])
        RED(T.sT[:], T.D2[:], A.add, r=["D2"], w=["sT"])
        CP(T.slu[:], T.sT[:], r=["sT"], w=["slu"])
        CP(T.Ow[:].indirect(T.slu[:]), T.ox[:], r=["slu", "ox"], w=["Ow", "Owd"])
        if not last:
            offcast(t + 1, T.Ow, "Ow")

        def finish(t=t, last=last):
            TT(T.ox[:], T.PG[:, 0:12, :], T.Ow[:, t:V:8], A.subtract, r=["b", "Ow"], w=["ox"], b=["PG"])
            TT(T.PG[:, 12:24, :], T.ox[:], T.PG[:, 12:24, :], A.mult, r=["ox", "oh"], w=["oy"], b=["PG"])
            TT(T.Ow[:, t:V:8], T.Ow[:, t:V:8], T.PG[:, 12:24, :], A.add, r=["Ow", "oy"], w=["Ow"], b=["PG"])
            if not last:
                RED(T.wc[:], T.w12[:], A.add, r=["w12"], w=["wc"])
                MM(T.PG[:, 24, 0:1], T.R0[:], T.wc[:], True, True, r=["R0", "wc"], w=["tot"], b=["PG"])

        if not last:
            pend.append(finish)
            continue
        for j, (bn, bk) in enumerate((("PX", T.PX), ("PE", T.PE), ("PB", T.PB))):
            MM(bk[:], T.Gc[:], T.W0[:, 512 * j:512 * j + 512], True, True, r=["Gc", "W0"], w=["yp%d" % j], b=[bn])
            SC(T.ycb[:, 512 * j:512 * j + 512], bk[:], r=["yp%d" % j], w=["yb%d" % j], b=[bn])
        op("s", lambda: g.scalar.dma_start(T.yc[:], T.ycb[0::16, :]), r=R("yb", 3), dma="dz", amt=16)
        finish()
        op("y", lambda: g.sync.dma_start(T.yo[:], T.Ow[:, 0:V]), r=["Ow"], dma="dy", amt=16)
    need("y", [(k, cnt[k]) for k in ("v", "t", "s", "p", "dc", "d0", "d1", "d2", "d3", "dh", "dx", "dw", "dy", "dz")])
    need("p", list(sem_of.values()) + list(nls.items()))
